import numpy as np
import ml_dtypes


def mxq(x, axis, fmt="e4m3"):
    dtype, down = {"e4m3": (ml_dtypes.float8_e4m3fn, 7), "e5m2": (ml_dtypes.float8_e5m2, 14)}[fmt]
    v = np.moveaxis(np.asarray(x, np.float32).astype(ml_dtypes.bfloat16).astype(np.float64), axis, -1)
    blocks = v.reshape(v.shape[:-1] + (-1, 32))
    amax = np.abs(blocks).max(-1, keepdims=True)
    byte = np.maximum(np.where(amax > 0, np.frexp(amax)[1] - 1 + 127, 0) - down, 1)
    scale = np.exp2(byte - 127.0)
    codes = (blocks / scale).astype(np.float32).astype(dtype).astype(np.float64)
    return np.moveaxis((codes * scale).reshape(v.shape), -1, axis)


WIDE = False


def mx_kscale(k):
    if not WIDE:
        return np.ones(k)
    levels = np.array([10, -10, 5, -5, 0])
    if k % 512:
        return np.exp2(np.random.permutation(np.resize(levels, k // 32))).repeat(32)
    a = np.empty((k // 512, 16))
    for p in range(k // 512):
        a[p, :8] = np.random.permutation(np.resize(levels, 8))
        for g in range(8):
            far = levels[np.abs(levels - a[p, g]) >= 10]
            a[p, g + 8] = far[np.random.randint(len(far))]
    return np.exp2(a.ravel()).repeat(32)


def f64(x):
    return np.asarray(x).astype(np.float64)


def striped(idx):
    return np.tile(idx.reshape(-1, 16).T, (8, 1)).astype(np.uint16)


def unstriped(offs):
    return offs[:16].T.reshape(-1).astype(np.int64)


def relu(v):
    return np.maximum(v, 0.0)


K, T, E, C, H, N = 1024, 512, 4, 256, 512, 256


def by_expert(wq, xq):
    return np.concatenate([wq[e].T @ xq[:, e * C:(e + 1) * C] for e in range(E)], axis=1)


def setup_inputs():
    n = np.random.standard_normal
    s = mx_kscale(K)[:, None]
    u = mx_kscale(H)
    first = np.random.permutation(np.repeat(np.arange(E), T // E))
    second = (first + 1 + np.random.permutation(np.repeat(np.arange(E - 1), -(-T // (E - 1)))[:T])) % E
    while np.bincount(second, minlength=E).max() != T // E:
        load = np.bincount(second, minlength=E); hi, lo = int(load.argmax()), int(load.argmin())
        t = np.flatnonzero((second == hi) & (first != lo))[0]; second[t] = lo
    slot_token = np.empty(E * C, np.int64); pos = np.empty((2, T), np.int64); fill = np.zeros(E, np.int64)
    place = np.stack([np.random.permutation(C) for _ in range(E)])
    for r, deal in enumerate((first, second)):
        for t in np.random.permutation(T):
            e = deal[t]; j = e * C + place[e, fill[e]]; fill[e] += 1; slot_token[j] = t; pos[r, t] = j
    g = np.random.uniform(0.2, 0.8, T)
    return {
        "xT": (n((K, T)) * s).astype(np.float32),
        "w1": (n((E, K, H)) / np.sqrt(K) / s[None] * u[None, None, :]).astype(np.float32),
        "w2": (n((E, H, N)) / np.sqrt(H) / u[None, :, None]).astype(np.float32),
        "gate": np.stack([np.tile(g, (N, 1)), np.tile(1.0 - g, (N, 1))]).astype(np.float32),
        "offs": striped(slot_token),
        "pos1": striped(pos[0]),
        "pos2": striped(pos[1]),
    }


def reference(xT, w1, w2, gate, offs, pos1, pos2):
    idx = unstriped(offs)
    xq = mxq(f64(xT)[:, idx], 0, "e4m3")
    h = relu(by_expert(mxq(f64(w1), 1, "e4m3"), xq))
    y = by_expert(mxq(f64(w2), 1, "e4m3"), mxq(h, 0, "e4m3"))
    return f64(gate[0]) * y[:, unstriped(pos1)] + f64(gate[1]) * y[:, unstriped(pos2)]

@@ -1,0 +1,331 @@
+from contextlib import ExitStack
+
+import concourse.mybir as mybir
+from concourse.masks import make_identity
+
+K, T, E, C, H, N = 1024, 512, 4, 256, 512, 256
+
+F32 = mybir.dt.float32
+BF16 = mybir.dt.bfloat16
+U32 = mybir.dt.uint32
+U16 = mybir.dt.uint16
+U8 = mybir.dt.uint8
+FP8X4 = mybir.dt.float8_e4m3fn_x4
+MULT = mybir.AluOpType.mult
+ADD = mybir.AluOpType.add
+RELU = mybir.ActivationFunctionType.Relu
+
+P = 128
+PACK = 4
+K_PASS = P * PACK
+PASSES = K // K_PASS
+HALF = C // 2
+N_BLOCKS = N // P
+SCALE_ROW = 4
+T_HALF = T // 2
+
+FLOPS = 2 * E * C * (K * H + H * N)
+
+X_VECTOR = 128
+W1_VECTOR = ((0, 48), (40, 56), (0, 96), (16, 112))
+GROUPS = ((0, 256), (256, 640), (640, 1024))
+WORD_TAGS = ("words0", "words1", "grouped10")
+SCALE_TAGS = ("slot_scales0", "slot_scales1", "raw11")
+
+
+def tile_routed_moe_kernel(tc, xT, w1, w2, gate, offs, pos1, pos2, out):
+    nc = tc.nc
+    with ExitStack() as ctx:
+        keep = ctx.enter_context(tc.tile_pool(name="keep", bufs=1))
+        psum_h = ctx.enter_context(tc.psum_pool(name="psum_h", bufs=4))
+        psum_y = ctx.enter_context(tc.psum_pool(name="psum_y", bufs=4))
+
+        offs_t = keep.tile([P, E * C // 16], U16, name="offs_t")
+        pos1_t = keep.tile([P, T // 16], U16, name="pos1_t")
+        pos2_t = keep.tile([P, T // 16], U16, name="pos2_t")
+        x_codes = [keep.tile([P, T], U32, align_bytes=64, name=f"x_codes{s}") for s in range(PASSES)]
+        x_scales = keep.tile([P, T], U8, align_bytes=64, name="x_scales")
+        y = [keep.tile([P, E * C], F32, name=f"y{b}") for b in range(N_BLOCKS)]
+        gates = [[keep.tile([P, T], F32, name=f"gate{r}_{b}") for b in range(N_BLOCKS)] for r in range(2)]
+        x_raw, x_grouped, words, slot_scales = {}, {}, {}, {}
+        w1_raw, w1_grouped, w1_codes, w1_scales = {}, {}, {}, {}
+        w2_raw, w2_grouped, w2_codes, w2_scales = {}, {}, {}, {}
+        h_grouped, h_codes, h_scales, h_acc, y_acc = {}, {}, {}, {}, {}
+
+        def load_x(s):
+            for part in range(2):
+                cols = slice(part * T_HALF, (part + 1) * T_HALF)
+                x_raw[s, part] = keep.tile([P, PACK, T_HALF], F32, name=f"x_raw{s}_{part}")
+                nc.sync.dma_start(
+                    out=x_raw[s, part][:],
+                    in_=xT[s * K_PASS : (s + 1) * K_PASS, cols].rearrange("(p j) n -> p j n", j=PACK),
+                )
+
+        def load_w1(e, s):
+            w1_raw[e, s] = keep.tile([P, PACK, H], F32, align_bytes=64, name=f"w1_raw{e}_{s}", tag=f"raw{e}{s}")
+            nc.sync.dma_start(
+                out=w1_raw[e, s][:], in_=w1[e, s * K_PASS : (s + 1) * K_PASS, :].rearrange("(p j) n -> p j n", j=PACK)
+            )
+
+        def load_w2(e):
+            w2_raw[e] = keep.tile([P, PACK, N], F32, name=f"w2_raw{e}")
+            nc.sync.dma_start(out=w2_raw[e][:], in_=w2[e, :, :].rearrange("(p j) n -> p j n", j=PACK))
+
+        def x_views(s, part, a, z):
+            first = part * T_HALF
+            return (
+                x_grouped[s][:, first + a : first + z, :].rearrange("p (c i) j -> p c j i", i=4),
+                x_raw[s, part][:, :, a:z].rearrange("p j (c i) -> p c j i", i=4),
+            )
+
+        def w1_views(e, s, a, z):
+            return (
+                w1_grouped[e, s][:, :, a:z, :].rearrange("p t m j -> p m j t"),
+                w1_raw[e, s][:, :, a * PACK : z * PACK].rearrange("p j (m t) -> p m j t", t=PACK),
+            )
+
+        def x_cast(s):
+            x_grouped[s] = keep.tile([P, T, PACK], BF16, align_bytes=64, name=f"x_grouped{s}")
+            for part in range(2):
+                dst, src = x_views(s, part, 0, X_VECTOR)
+                nc.vector.tensor_copy(dst, src)
+                dst, src = x_views(s, part, X_VECTOR, T_HALF)
+                nc.scalar.copy(dst, src)
+
+        def x_quantize(s):
+            nc.vector.quantize_mx(
+                out=x_codes[s][:].bitcast(FP8X4),
+                scales=x_scales[s * SCALE_ROW :, :],
+                in_=x_grouped[s][:].rearrange("p n j -> p (n j)"),
+            )
+
+        def picks(group):
+            return offs_t[:, GROUPS[group][0] // 16 : GROUPS[group][1] // 16]
+
+        def gather_words(group, s):
+            if s == 0:
+                size = GROUPS[group][1] - GROUPS[group][0]
+                words[group] = keep.tile(
+                    [P, PASSES, size], U32, align_bytes=64, name=f"words{group}", tag=WORD_TAGS[group]
+                )
+            nc.vector.tensor_copy(words[group][:, s, :], x_codes[s][:].indirect(picks(group)))
+
+        def gather_scales(group):
+            size = GROUPS[group][1] - GROUPS[group][0]
+            slot_scales[group] = keep.tile(
+                [P, size], U8, align_bytes=64, name=f"slot_scales{group}", tag=SCALE_TAGS[group]
+            )
+            nc.vector.tensor_copy(slot_scales[group][:], x_scales[:].indirect(picks(group)))
+
+        def w1_cast(e, s):
+            w1_grouped[e, s] = keep.tile(
+                [P, PACK, P, PACK], BF16, align_bytes=64, name=f"w1_grouped{e}_{s}", tag=f"grouped{e}{s}"
+            )
+            split = W1_VECTOR[e][s]
+            if split > 0:
+                dst, src = w1_views(e, s, 0, split)
+                nc.vector.tensor_copy(dst, src)
+            if split < P:
+                dst, src = w1_views(e, s, split, P)
+                nc.scalar.copy(dst, src)
+
+        def w1_quantize(e, s):
+            w1_codes[e, s] = keep.tile([P, H], U32, align_bytes=64, name=f"w1_codes{e}_{s}")
+            w1_scales[e, s] = keep.tile([P, H], U8, align_bytes=64, name=f"w1_scales{e}_{s}")
+            nc.vector.quantize_mx(
+                out=w1_codes[e, s][:].bitcast(FP8X4),
+                scales=w1_scales[e, s][:],
+                in_=w1_grouped[e, s][:].rearrange("p t m j -> p (t m j)"),
+            )
+
+        def w2_cast(e, engine_copy):
+            w2_grouped[e] = keep.tile([P, N, PACK], BF16, align_bytes=64, name=f"w2_grouped{e}")
+            engine_copy(
+                w2_grouped[e][:].rearrange("p (c i) j -> p c j i", i=4),
+                w2_raw[e][:].rearrange("p j (c i) -> p c j i", i=4),
+            )
+
+        def w2_quantize(e):
+            w2_codes[e] = keep.tile([P, N], U32, align_bytes=64, name=f"w2_codes{e}")
+            w2_scales[e] = keep.tile([P, N], U8, align_bytes=64, name=f"w2_scales{e}")
+            nc.vector.quantize_mx(
+                out=w2_codes[e][:].bitcast(FP8X4), scales=w2_scales[e][:], in_=w2_grouped[e][:].rearrange("p n j -> p (n j)")
+            )
+
+        def first_matmul(e):
+            for half in range(2):
+                slot = e * C + half * HALF
+                group = [g for g in range(len(GROUPS)) if GROUPS[g][0] <= slot < GROUPS[g][1]][0]
+                cols = slice(slot - GROUPS[group][0], slot - GROUPS[group][0] + HALF)
+                acc = psum_h.tile([P, PACK, HALF], F32, name="h_acc")
+                for t in range(PACK):
+                    rows = slice(t * P, (t + 1) * P)
+                    for s in range(PASSES):
+                        nc.tensor.matmul_mx(
+                            out=acc[:, t, :],
+                            lhsT=w1_codes[e, s][:, rows].bitcast(FP8X4),
+                            lhsT_scale=w1_scales[e, s][:, rows],
+                            rhs=words[group][:, s, cols].bitcast(FP8X4),
+                            rhs_scale=slot_scales[group][s * SCALE_ROW :, cols],
+                            start=(s == 0),
+                            stop=(s == PASSES - 1),
+                        )
+                h_acc[e, half] = acc
+
+        def h_tile(e):
+            tag = f"raw{e + 1}0" if e < E - 1 else "h_grouped_last"
+            h_grouped[e] = keep.tile([P, C, PACK], BF16, align_bytes=64, name=f"h_grouped{e}", tag=tag)
+
+        def relu_scalar(e, half):
+            nc.scalar.activation(
+                h_grouped[e][:, half * HALF : (half + 1) * HALF, :], h_acc[e, half][:].rearrange("p t n -> p n t"), RELU
+            )
+
+        def relu_vector(e, half):
+            nc.vector.tensor_scalar_max(
+                h_grouped[e][:, half * HALF : (half + 1) * HALF, :], h_acc[e, half][:].rearrange("p t n -> p n t"), 0.0
+            )
+
+        def h_quantize(e, a, z):
+            if a == 0:
+                h_codes[e] = keep.tile([P, C], U32, align_bytes=64, name=f"h_codes{e}")
+                h_scales[e] = keep.tile([P, C], U8, align_bytes=64, name=f"h_scales{e}")
+            nc.vector.quantize_mx(
+                out=h_codes[e][:, a:z].bitcast(FP8X4),
+                scales=h_scales[e][:, a:z],
+                in_=h_grouped[e][:, a:z, :].rearrange("p n t -> p (n t)"),
+            )
+
+        def second_matmul(e):
+            for b in range(N_BLOCKS):
+                acc = psum_y.tile([P, T], F32, name="y_acc")
+                nc.tensor.matmul_mx(
+                    out=acc[:, :C],
+                    lhsT=w2_codes[e][:, b * P : (b + 1) * P].bitcast(FP8X4),
+                    lhsT_scale=w2_scales[e][:, b * P : (b + 1) * P],
+                    rhs=h_codes[e][:].bitcast(FP8X4),
+                    rhs_scale=h_scales[e][:],
+                    start=True,
+                    stop=True,
+                )
+                y_acc[e, b] = acc
+
+        def y_copy(e, b, engine_copy):
+            engine_copy(y[b][:, e * C : (e + 1) * C], y_acc[e, b][:, :C])
+
+        nc.gpsimd.memset(x_scales[:], 0)
+        identity = keep.tile([P, P], F32, name="identity")
+        make_identity(nc, identity[:])
+
+        load_x(0)
+        nc.sync.dma_start(out=offs_t[:], in_=offs)
+        load_x(1)
+        load_w1(0, 0)
+        load_w1(0, 1)
+        load_w1(1, 0)
+        load_w1(1, 1)
+        load_w1(2, 0)
+        load_w2(0)
+        nc.sync.dma_start(out=pos1_t[:], in_=pos1)
+        nc.sync.dma_start(out=pos2_t[:], in_=pos2)
+        load_w1(2, 1)
+        load_w2(3)
+        load_w1(3, 0)
+        load_w2(1)
+        load_w1(3, 1)
+        load_w2(2)
+        for b in range(N_BLOCKS):
+            for r in range(2):
+                nc.sync.dma_start(out=gates[r][b][:], in_=gate[r, b * P : (b + 1) * P, :])
+
+        x_cast(0)
+        x_quantize(0)
+        x_cast(1)
+        gather_words(0, 0)
+        x_quantize(1)
+
+        w1_cast(0, 0)
+        gather_words(0, 1)
+        gather_scales(0)
+        w1_quantize(0, 0)
+        w1_cast(0, 1)
+        gather_words(1, 0)
+        w1_quantize(0, 1)
+        first_matmul(0)
+
+        w1_cast(1, 0)
+        gather_words(1, 1)
+        gather_scales(1)
+        h_tile(0)
+        relu_scalar(0, 0)
+        relu_scalar(0, 1)
+        w1_quantize(1, 0)
+        w1_cast(1, 1)
+        h_quantize(0, 0, C)
+        w1_quantize(1, 1)
+        first_matmul(1)
+
+        w1_cast(2, 0)
+        w2_cast(0, nc.vector.tensor_copy)
+        gather_words(2, 0)
+        gather_words(2, 1)
+        gather_scales(2)
+        h_tile(1)
+        relu_scalar(1, 0)
+        relu_scalar(1, 1)
+        w2_quantize(0)
+        second_matmul(0)
+        w1_quantize(2, 0)
+        y_copy(0, 0, nc.scalar.copy)
+        y_copy(0, 1, nc.scalar.copy)
+        w1_cast(2, 1)
+        h_quantize(1, 0, C)
+        w1_quantize(2, 1)
+        first_matmul(2)
+
+        w1_cast(3, 0)
+        w2_cast(1, nc.vector.tensor_copy)
+        h_tile(2)
+        relu_scalar(2, 0)
+        relu_scalar(2, 1)
+        w2_quantize(1)
+        second_matmul(1)
+        w1_quantize(3, 0)
+        y_copy(1, 0, nc.scalar.copy)
+        y_copy(1, 1, nc.scalar.copy)
+        w1_cast(3, 1)
+        h_quantize(2, 0, C)
+        w1_quantize(3, 1)
+        first_matmul(3)
+
+        w2_cast(2, nc.vector.tensor_copy)
+        w2_cast(3, nc.vector.tensor_copy)
+        w2_quantize(2)
+        h_tile(3)
+        relu_scalar(3, 0)
+        relu_vector(3, 1)
+        second_matmul(2)
+        w2_quantize(3)
+        h_quantize(3, 0, HALF)
+        h_quantize(3, HALF, C)
+        y_copy(2, 0, nc.scalar.copy)
+        y_copy(2, 1, nc.scalar.copy)
+        second_matmul(3)
+        y_copy(3, 0, nc.vector.tensor_copy)
+        y_copy(3, 1, nc.scalar.copy)
+
+        for b in range(N_BLOCKS):
+            picked = []
+            for r, places in enumerate((pos1_t, pos2_t)):
+                pick = keep.tile([P, T], F32, name=f"pick{r}_{b}")
+                nc.vector.tensor_tensor(pick[:], y[b][:].indirect(places[:]), gates[r][b][:], MULT)
+                picked.append(pick)
+            total = keep.tile([P, T], F32, name=f"total{b}")
+            if b == 0:
+                acc = psum_y.tile([P, T], F32, name="y_acc")
+                nc.tensor.matmul(acc[:], identity[:], picked[0][:], start=True, stop=False)
+                nc.tensor.matmul(acc[:], identity[:], picked[1][:], start=False, stop=True)
+                nc.scalar.copy(total[:], acc[:])
+            else:
+                nc.vector.tensor_tensor(total[:], picked[0][:], picked[1][:], ADD)
+            nc.sync.dma_start(out=out[b * P : (b + 1) * P, :], in_=total[:])

@@ -26,11 +26,12 @@ T_HALF = T // 2
 
 FLOPS = 2 * E * C * (K * H + H * N)
 
-X_VECTOR = 128
-W1_VECTOR = ((0, 48), (40, 56), (0, 96), (16, 112))
+X_VECTOR = 144
+W1_VECTOR = ((0, 0), (0, 16), (80, 96), (0, 0))
+W2_VECTOR = (256, 256, 160, 96)
 GROUPS = ((0, 256), (256, 640), (640, 1024))
-WORD_TAGS = ("words0", "words1", "grouped10")
-SCALE_TAGS = ("slot_scales0", "slot_scales1", "raw11")
+WORD_TAGS = ("words0", "grouped00", "grouped01")
+SCALE_TAGS = ("slot_scales0", "slot_scales1", "slot_scales2")
 
 
 def tile_routed_moe_kernel(tc, xT, w1, w2, gate, offs, pos1, pos2, out):
@@ -46,20 +47,17 @@ def tile_routed_moe_kernel(tc, xT, w1, w2, gate, offs, pos1, pos2, out):
         x_codes = [keep.tile([P, T], U32, align_bytes=64, name=f"x_codes{s}") for s in range(PASSES)]
         x_scales = keep.tile([P, T], U8, align_bytes=64, name="x_scales")
         y = [keep.tile([P, E * C], F32, name=f"y{b}") for b in range(N_BLOCKS)]
-        gates = [[keep.tile([P, T], F32, name=f"gate{r}_{b}") for b in range(N_BLOCKS)] for r in range(2)]
+        gates = [keep.tile([P, 2, T], F32, name=f"gates{b}") for b in range(N_BLOCKS)]
         x_raw, x_grouped, words, slot_scales = {}, {}, {}, {}
         w1_raw, w1_grouped, w1_codes, w1_scales = {}, {}, {}, {}
         w2_raw, w2_grouped, w2_codes, w2_scales = {}, {}, {}, {}
         h_grouped, h_codes, h_scales, h_acc, y_acc = {}, {}, {}, {}, {}
 
-        def load_x(s):
-            for part in range(2):
-                cols = slice(part * T_HALF, (part + 1) * T_HALF)
-                x_raw[s, part] = keep.tile([P, PACK, T_HALF], F32, name=f"x_raw{s}_{part}")
-                nc.sync.dma_start(
-                    out=x_raw[s, part][:],
-                    in_=xT[s * K_PASS : (s + 1) * K_PASS, cols].rearrange("(p j) n -> p j n", j=PACK),
-                )
+        def load_x(s, a, z):
+            x_raw[s, a] = keep.tile([P, PACK, z - a], F32, name=f"x_raw{s}_{a}")
+            nc.sync.dma_start(
+                out=x_raw[s, a][:], in_=xT[s * K_PASS : (s + 1) * K_PASS, a:z].rearrange("(p j) n -> p j n", j=PACK)
+            )
 
         def load_w1(e, s):
             w1_raw[e, s] = keep.tile([P, PACK, H], F32, align_bytes=64, name=f"w1_raw{e}_{s}", tag=f"raw{e}{s}")
@@ -71,11 +69,11 @@ def tile_routed_moe_kernel(tc, xT, w1, w2, gate, offs, pos1, pos2, out):
             w2_raw[e] = keep.tile([P, PACK, N], F32, name=f"w2_raw{e}")
             nc.sync.dma_start(out=w2_raw[e][:], in_=w2[e, :, :].rearrange("(p j) n -> p j n", j=PACK))
 
-        def x_views(s, part, a, z):
-            first = part * T_HALF
+        def x_views(s, a, z):
+            start = max(first for key, first in x_raw if key == s and first <= a)
             return (
-                x_grouped[s][:, first + a : first + z, :].rearrange("p (c i) j -> p c j i", i=4),
-                x_raw[s, part][:, :, a:z].rearrange("p j (c i) -> p c j i", i=4),
+                x_grouped[s][:, a:z, :].rearrange("p (c i) j -> p c j i", i=4),
+                x_raw[s, start][:, :, a - start : z - start].rearrange("p j (c i) -> p c j i", i=4),
             )
 
         def w1_views(e, s, a, z):
@@ -86,10 +84,10 @@ def tile_routed_moe_kernel(tc, xT, w1, w2, gate, offs, pos1, pos2, out):
 
         def x_cast(s):
             x_grouped[s] = keep.tile([P, T, PACK], BF16, align_bytes=64, name=f"x_grouped{s}")
-            for part in range(2):
-                dst, src = x_views(s, part, 0, X_VECTOR)
+            for a in (0, T_HALF):
+                dst, src = x_views(s, a, a + X_VECTOR)
                 nc.vector.tensor_copy(dst, src)
-                dst, src = x_views(s, part, X_VECTOR, T_HALF)
+                dst, src = x_views(s, a + X_VECTOR, a + T_HALF)
                 nc.scalar.copy(dst, src)
 
         def x_quantize(s):
@@ -138,12 +136,19 @@ def tile_routed_moe_kernel(tc, xT, w1, w2, gate, offs, pos1, pos2, out):
                 in_=w1_grouped[e, s][:].rearrange("p t m j -> p (t m j)"),
             )
 
-        def w2_cast(e, engine_copy):
+        def w2_cast(e):
             w2_grouped[e] = keep.tile([P, N, PACK], BF16, align_bytes=64, name=f"w2_grouped{e}")
-            engine_copy(
-                w2_grouped[e][:].rearrange("p (c i) j -> p c j i", i=4),
-                w2_raw[e][:].rearrange("p j (c i) -> p c j i", i=4),
-            )
+            split = W2_VECTOR[e]
+            if split > 0:
+                nc.vector.tensor_copy(
+                    w2_grouped[e][:, :split, :].rearrange("p (c i) j -> p c j i", i=4),
+                    w2_raw[e][:, :, :split].rearrange("p j (c i) -> p c j i", i=4),
+                )
+            if split < N:
+                nc.scalar.copy(
+                    w2_grouped[e][:, split:, :].rearrange("p (c i) j -> p c j i", i=4),
+                    w2_raw[e][:, :, split:].rearrange("p j (c i) -> p c j i", i=4),
+                )
 
         def w2_quantize(e):
             w2_codes[e] = keep.tile([P, N], U32, align_bytes=64, name=f"w2_codes{e}")
@@ -172,8 +177,7 @@ def tile_routed_moe_kernel(tc, xT, w1, w2, gate, offs, pos1, pos2, out):
                         )
                 h_acc[e, half] = acc
 
-        def h_tile(e):
-            tag = f"raw{e + 1}0" if e < E - 1 else "h_grouped_last"
+        def h_tile(e, tag):
             h_grouped[e] = keep.tile([P, C, PACK], BF16, align_bytes=64, name=f"h_grouped{e}", tag=tag)
 
         def relu_scalar(e, half):
@@ -198,9 +202,13 @@ def tile_routed_moe_kernel(tc, xT, w1, w2, gate, offs, pos1, pos2, out):
 
         def second_matmul(e):
             for b in range(N_BLOCKS):
-                acc = psum_y.tile([P, T], F32, name="y_acc")
+                if e == 1:
+                    bank = y_acc[0, b]
+                else:
+                    bank = psum_y.tile([P, 2, C], F32, name="y_acc")
+                y_acc[e, b] = bank
                 nc.tensor.matmul_mx(
-                    out=acc[:, :C],
+                    out=bank[:, e % 2, :],
                     lhsT=w2_codes[e][:, b * P : (b + 1) * P].bitcast(FP8X4),
                     lhsT_scale=w2_scales[e][:, b * P : (b + 1) * P],
                     rhs=h_codes[e][:].bitcast(FP8X4),
@@ -208,42 +216,43 @@ def tile_routed_moe_kernel(tc, xT, w1, w2, gate, offs, pos1, pos2, out):
                     start=True,
                     stop=True,
                 )
-                y_acc[e, b] = acc
 
-        def y_copy(e, b, engine_copy):
-            engine_copy(y[b][:, e * C : (e + 1) * C], y_acc[e, b][:, :C])
+        def y_copy(e, count, b, engine_copy):
+            engine_copy(
+                y[b][:, e * C : (e + count) * C],
+                y_acc[e, b][:, e % 2 : e % 2 + count, :].rearrange("p e n -> p (e n)"),
+            )
 
         nc.gpsimd.memset(x_scales[:], 0)
         identity = keep.tile([P, P], F32, name="identity")
         make_identity(nc, identity[:])
 
-        load_x(0)
+        load_x(0, 0, T_HALF)
         nc.sync.dma_start(out=offs_t[:], in_=offs)
-        load_x(1)
+        load_x(0, T_HALF, T)
+        load_x(1, 0, T)
         load_w1(0, 0)
         load_w1(0, 1)
         load_w1(1, 0)
         load_w1(1, 1)
+        load_w2(2)
         load_w1(2, 0)
-        load_w2(0)
-        nc.sync.dma_start(out=pos1_t[:], in_=pos1)
-        nc.sync.dma_start(out=pos2_t[:], in_=pos2)
         load_w1(2, 1)
-        load_w2(3)
         load_w1(3, 0)
         load_w2(1)
+        nc.sync.dma_start(out=pos1_t[:], in_=pos1)
+        nc.sync.dma_start(out=pos2_t[:], in_=pos2)
         load_w1(3, 1)
-        load_w2(2)
+        load_w2(3)
+        load_w2(0)
         for b in range(N_BLOCKS):
-            for r in range(2):
-                nc.sync.dma_start(out=gates[r][b][:], in_=gate[r, b * P : (b + 1) * P, :])
+            nc.sync.dma_start(out=gates[b][:], in_=gate[:, b * P : (b + 1) * P, :].rearrange("r p t -> p r t"))
 
         x_cast(0)
         x_quantize(0)
         x_cast(1)
         gather_words(0, 0)
         x_quantize(1)
-
         w1_cast(0, 0)
         gather_words(0, 1)
         gather_scales(0)
@@ -252,73 +261,67 @@ def tile_routed_moe_kernel(tc, xT, w1, w2, gate, offs, pos1, pos2, out):
         gather_words(1, 0)
         w1_quantize(0, 1)
         first_matmul(0)
-
         w1_cast(1, 0)
         gather_words(1, 1)
         gather_scales(1)
-        h_tile(0)
-        relu_scalar(0, 0)
-        relu_scalar(0, 1)
         w1_quantize(1, 0)
         w1_cast(1, 1)
-        h_quantize(0, 0, C)
-        w1_quantize(1, 1)
-        first_matmul(1)
-
-        w1_cast(2, 0)
-        w2_cast(0, nc.vector.tensor_copy)
+        h_tile(0, "raw11")
+        relu_scalar(0, 0)
+        relu_scalar(0, 1)
         gather_words(2, 0)
         gather_words(2, 1)
         gather_scales(2)
-        h_tile(1)
+        h_quantize(0, 0, C)
+        w1_quantize(1, 1)
+        first_matmul(1)
+        w1_cast(2, 0)
+        h_tile(1, "raw20")
         relu_scalar(1, 0)
-        relu_scalar(1, 1)
-        w2_quantize(0)
-        second_matmul(0)
+        relu_vector(1, 1)
         w1_quantize(2, 0)
-        y_copy(0, 0, nc.scalar.copy)
-        y_copy(0, 1, nc.scalar.copy)
         w1_cast(2, 1)
         h_quantize(1, 0, C)
         w1_quantize(2, 1)
         first_matmul(2)
-
+        w2_cast(2)
+        w2_quantize(2)
         w1_cast(3, 0)
-        w2_cast(1, nc.vector.tensor_copy)
-        h_tile(2)
+        w1_quantize(3, 0)
+        w1_cast(3, 1)
+        h_tile(2, "raw31")
         relu_scalar(2, 0)
         relu_scalar(2, 1)
-        w2_quantize(1)
-        second_matmul(1)
-        w1_quantize(3, 0)
-        y_copy(1, 0, nc.scalar.copy)
-        y_copy(1, 1, nc.scalar.copy)
-        w1_cast(3, 1)
         h_quantize(2, 0, C)
         w1_quantize(3, 1)
         first_matmul(3)
-
-        w2_cast(2, nc.vector.tensor_copy)
-        w2_cast(3, nc.vector.tensor_copy)
-        w2_quantize(2)
-        h_tile(3)
+        w2_cast(0)
+        w2_quantize(0)
+        w2_cast(1)
+        w2_quantize(1)
+        w2_cast(3)
+        h_tile(3, "h_grouped3")
         relu_scalar(3, 0)
-        relu_vector(3, 1)
+        relu_scalar(3, 1)
+        second_matmul(0)
+        second_matmul(1)
+        y_copy(0, 2, 0, nc.scalar.copy)
+        y_copy(0, 2, 1, nc.scalar.copy)
         second_matmul(2)
         w2_quantize(3)
         h_quantize(3, 0, HALF)
         h_quantize(3, HALF, C)
-        y_copy(2, 0, nc.scalar.copy)
-        y_copy(2, 1, nc.scalar.copy)
+        y_copy(2, 1, 0, nc.scalar.copy)
+        y_copy(2, 1, 1, nc.scalar.copy)
         second_matmul(3)
-        y_copy(3, 0, nc.vector.tensor_copy)
-        y_copy(3, 1, nc.scalar.copy)
+        y_copy(3, 1, 0, nc.vector.tensor_copy)
+        y_copy(3, 1, 1, nc.scalar.copy)
 
         for b in range(N_BLOCKS):
             picked = []
             for r, places in enumerate((pos1_t, pos2_t)):
                 pick = keep.tile([P, T], F32, name=f"pick{r}_{b}")
-                nc.vector.tensor_tensor(pick[:], y[b][:].indirect(places[:]), gates[r][b][:], MULT)
+                nc.vector.tensor_tensor(pick[:], y[b][:].indirect(places[:]), gates[b][:, r, :], MULT)
                 picked.append(pick)
             total = keep.tile([P, T], F32, name=f"total{b}")
             if b == 0:

@@ -26,12 +26,13 @@ T_HALF = T // 2
 
 FLOPS = 2 * E * C * (K * H + H * N)
 
-X_VECTOR = 144
-W1_VECTOR = ((0, 0), (0, 16), (80, 96), (0, 0))
-W2_VECTOR = (256, 256, 160, 96)
-GROUPS = ((0, 256), (256, 640), (640, 1024))
+PE_SUMS = 320
+X_VECTOR = 160
+W1_VECTOR = ((0, 0), (24, 24), (64, 40), (48, 80))
+W2_VECTOR = (96, 160, 96, 128)
+GROUPS = ((0, 384), (384, 768), (768, 1024))
 WORD_TAGS = ("words0", "grouped00", "grouped01")
-SCALE_TAGS = ("slot_scales0", "slot_scales1", "slot_scales2")
+SCALE_TAGS = ("slot_scales0", "slot_scales1", "raw01")
 
 
 def tile_routed_moe_kernel(tc, xT, w1, w2, gate, offs, pos1, pos2, out):
@@ -200,19 +201,16 @@ def tile_routed_moe_kernel(tc, xT, w1, w2, gate, offs, pos1, pos2, out):
                 in_=h_grouped[e][:, a:z, :].rearrange("p n t -> p (n t)"),
             )
 
-        def second_matmul(e):
+        def second_matmul(e, a, z):
             for b in range(N_BLOCKS):
-                if e == 1:
-                    bank = y_acc[0, b]
-                else:
-                    bank = psum_y.tile([P, 2, C], F32, name="y_acc")
-                y_acc[e, b] = bank
+                if (e, b) not in y_acc:
+                    y_acc[e, b] = y_acc[0, b] if e == 1 else psum_y.tile([P, 2, C], F32, name="y_acc")
                 nc.tensor.matmul_mx(
-                    out=bank[:, e % 2, :],
+                    out=y_acc[e, b][:, e % 2, a:z],
                     lhsT=w2_codes[e][:, b * P : (b + 1) * P].bitcast(FP8X4),
                     lhsT_scale=w2_scales[e][:, b * P : (b + 1) * P],
-                    rhs=h_codes[e][:].bitcast(FP8X4),
-                    rhs_scale=h_scales[e][:],
+                    rhs=h_codes[e][:, a:z].bitcast(FP8X4),
+                    rhs_scale=h_scales[e][:, a:z],
                     start=True,
                     stop=True,
                 )
@@ -235,16 +233,16 @@ def tile_routed_moe_kernel(tc, xT, w1, w2, gate, offs, pos1, pos2, out):
         load_w1(0, 1)
         load_w1(1, 0)
         load_w1(1, 1)
-        load_w2(2)
+        load_w2(0)
         load_w1(2, 0)
         load_w1(2, 1)
+        load_w2(2)
         load_w1(3, 0)
-        load_w2(1)
         nc.sync.dma_start(out=pos1_t[:], in_=pos1)
         nc.sync.dma_start(out=pos2_t[:], in_=pos2)
         load_w1(3, 1)
+        load_w2(1)
         load_w2(3)
-        load_w2(0)
         for b in range(N_BLOCKS):
             nc.sync.dma_start(out=gates[b][:], in_=gate[:, b * P : (b + 1) * P, :].rearrange("r p t -> p r t"))
 
@@ -267,7 +265,7 @@ def tile_routed_moe_kernel(tc, xT, w1, w2, gate, offs, pos1, pos2, out):
         w1_quantize(1, 0)
         w1_cast(1, 1)
         h_tile(0, "raw11")
-        relu_scalar(0, 0)
+        relu_vector(0, 0)
         relu_scalar(0, 1)
         gather_words(2, 0)
         gather_words(2, 1)
@@ -275,17 +273,22 @@ def tile_routed_moe_kernel(tc, xT, w1, w2, gate, offs, pos1, pos2, out):
         h_quantize(0, 0, C)
         w1_quantize(1, 1)
         first_matmul(1)
+        w2_cast(1)
+        w2_quantize(1)
+        w2_cast(2)
+        w2_quantize(2)
         w1_cast(2, 0)
-        h_tile(1, "raw20")
-        relu_scalar(1, 0)
-        relu_vector(1, 1)
         w1_quantize(2, 0)
         w1_cast(2, 1)
+        h_tile(1, "raw21")
+        relu_vector(1, 0)
+        relu_scalar(1, 1)
         h_quantize(1, 0, C)
         w1_quantize(2, 1)
         first_matmul(2)
-        w2_cast(2)
-        w2_quantize(2)
+        w2_cast(0)
+        w2_quantize(0)
+        second_matmul(0, 0, C)
         w1_cast(3, 0)
         w1_quantize(3, 0)
         w1_cast(3, 1)
@@ -295,40 +298,50 @@ def tile_routed_moe_kernel(tc, xT, w1, w2, gate, offs, pos1, pos2, out):
         h_quantize(2, 0, C)
         w1_quantize(3, 1)
         first_matmul(3)
-        w2_cast(0)
-        w2_quantize(0)
-        w2_cast(1)
-        w2_quantize(1)
         w2_cast(3)
         h_tile(3, "h_grouped3")
         relu_scalar(3, 0)
-        relu_scalar(3, 1)
-        second_matmul(0)
-        second_matmul(1)
+        relu_vector(3, 1)
+        second_matmul(1, 0, C)
         y_copy(0, 2, 0, nc.scalar.copy)
         y_copy(0, 2, 1, nc.scalar.copy)
-        second_matmul(2)
+        second_matmul(2, 0, C)
         w2_quantize(3)
         h_quantize(3, 0, HALF)
+        second_matmul(3, 0, HALF)
         h_quantize(3, HALF, C)
+        second_matmul(3, HALF, C)
         y_copy(2, 1, 0, nc.scalar.copy)
         y_copy(2, 1, 1, nc.scalar.copy)
-        second_matmul(3)
         y_copy(3, 1, 0, nc.vector.tensor_copy)
         y_copy(3, 1, 1, nc.scalar.copy)
 
-        for b in range(N_BLOCKS):
-            picked = []
-            for r, places in enumerate((pos1_t, pos2_t)):
-                pick = keep.tile([P, T], F32, name=f"pick{r}_{b}")
-                nc.vector.tensor_tensor(pick[:], y[b][:].indirect(places[:]), gates[b][:, r, :], MULT)
-                picked.append(pick)
-            total = keep.tile([P, T], F32, name=f"total{b}")
-            if b == 0:
-                acc = psum_y.tile([P, T], F32, name="y_acc")
-                nc.tensor.matmul(acc[:], identity[:], picked[0][:], start=True, stop=False)
-                nc.tensor.matmul(acc[:], identity[:], picked[1][:], start=False, stop=True)
-                nc.scalar.copy(total[:], acc[:])
-            else:
-                nc.vector.tensor_tensor(total[:], picked[0][:], picked[1][:], ADD)
-            nc.sync.dma_start(out=out[b * P : (b + 1) * P, :], in_=total[:])
+        picked = {}
+
+        def pick(b, r, a, z):
+            places = (pos1_t, pos2_t)[r]
+            picked[b, r, a] = keep.tile([P, z - a], F32, name=f"picked{b}_{r}_{a}")
+            nc.vector.tensor_tensor(
+                picked[b, r, a][:], y[b][:].indirect(places[:, a // 16 : z // 16]), gates[b][:, r, a:z], MULT
+            )
+
+        pick(0, 0, 0, T)
+        pick(0, 1, 0, T)
+        total = keep.tile([P, T], F32, name="total0")
+        acc = psum_y.tile([P, T], F32, name="y_acc")
+        nc.tensor.matmul(acc[:, :PE_SUMS], identity[:], picked[0, 0, 0][:, :PE_SUMS], start=True, stop=False)
+        nc.tensor.matmul(acc[:, :PE_SUMS], identity[:], picked[0, 1, 0][:, :PE_SUMS], start=False, stop=True)
+        nc.scalar.copy(total[:, :PE_SUMS], acc[:, :PE_SUMS])
+        nc.vector.tensor_tensor(
+            total[:, PE_SUMS:], picked[0, 0, 0][:, PE_SUMS:], picked[0, 1, 0][:, PE_SUMS:], ADD
+        )
+        nc.sync.dma_start(out=out[:P, :], in_=total[:])
+
+        pick(1, 0, 0, T)
+        halves = ((0, T_HALF), (T_HALF, T))
+        for a, z in halves:
+            pick(1, 1, a, z)
+        for a, z in halves:
+            total = keep.tile([P, T_HALF], F32, name=f"total1_{a}")
+            nc.vector.tensor_tensor(total[:], picked[1, 0, 0][:, a:z], picked[1, 1, a][:], ADD)
+            nc.sync.dma_start(out=out[P:, a:z], in_=total[:])

from contextlib import ExitStack

import concourse.mybir as mybir
from concourse.masks import make_identity

K, T, E, C, H, N = 1024, 512, 4, 256, 512, 256

F32 = mybir.dt.float32
BF16 = mybir.dt.bfloat16
U32 = mybir.dt.uint32
U16 = mybir.dt.uint16
U8 = mybir.dt.uint8
FP8X4 = mybir.dt.float8_e4m3fn_x4
MULT = mybir.AluOpType.mult
ADD = mybir.AluOpType.add
RELU = mybir.ActivationFunctionType.Relu

P = 128
PACK = 4
K_PASS = P * PACK
PASSES = K // K_PASS
HALF = C // 2
N_BLOCKS = N // P
SCALE_ROW = 4
T_HALF = T // 2

FLOPS = 2 * E * C * (K * H + H * N)

PE_SUMS = 320
X_VECTOR = 160
W1_VECTOR = ((0, 0), (24, 24), (64, 40), (48, 80))
W2_VECTOR = (96, 160, 96, 128)
GROUPS = ((0, 384), (384, 768), (768, 1024))
WORD_TAGS = ("words0", "grouped00", "grouped01")
SCALE_TAGS = ("slot_scales0", "slot_scales1", "raw01")


def tile_routed_moe_kernel(tc, xT, w1, w2, gate, offs, pos1, pos2, out):
    nc = tc.nc
    with ExitStack() as ctx:
        keep = ctx.enter_context(tc.tile_pool(name="keep", bufs=1))
        psum_h = ctx.enter_context(tc.psum_pool(name="psum_h", bufs=4))
        psum_y = ctx.enter_context(tc.psum_pool(name="psum_y", bufs=4))

        offs_t = keep.tile([P, E * C // 16], U16, name="offs_t")
        pos1_t = keep.tile([P, T // 16], U16, name="pos1_t")
        pos2_t = keep.tile([P, T // 16], U16, name="pos2_t")
        x_codes = [keep.tile([P, T], U32, align_bytes=64, name=f"x_codes{s}") for s in range(PASSES)]
        x_scales = keep.tile([P, T], U8, align_bytes=64, name="x_scales")
        y = [keep.tile([P, E * C], F32, name=f"y{b}") for b in range(N_BLOCKS)]
        gates = [keep.tile([P, 2, T], F32, name=f"gates{b}") for b in range(N_BLOCKS)]
        x_raw, x_grouped, words, slot_scales = {}, {}, {}, {}
        w1_raw, w1_grouped, w1_codes, w1_scales = {}, {}, {}, {}
        w2_raw, w2_grouped, w2_codes, w2_scales = {}, {}, {}, {}
        h_grouped, h_codes, h_scales, h_acc, y_acc = {}, {}, {}, {}, {}

        def load_x(s, a, z):
            x_raw[s, a] = keep.tile([P, PACK, z - a], F32, name=f"x_raw{s}_{a}")
            nc.sync.dma_start(
                out=x_raw[s, a][:], in_=xT[s * K_PASS : (s + 1) * K_PASS, a:z].rearrange("(p j) n -> p j n", j=PACK)
            )

        def load_w1(e, s):
            w1_raw[e, s] = keep.tile([P, PACK, H], F32, align_bytes=64, name=f"w1_raw{e}_{s}", tag=f"raw{e}{s}")
            nc.sync.dma_start(
                out=w1_raw[e, s][:], in_=w1[e, s * K_PASS : (s + 1) * K_PASS, :].rearrange("(p j) n -> p j n", j=PACK)
            )

        def load_w2(e):
            w2_raw[e] = keep.tile([P, PACK, N], F32, name=f"w2_raw{e}")
            nc.sync.dma_start(out=w2_raw[e][:], in_=w2[e, :, :].rearrange("(p j) n -> p j n", j=PACK))

        def x_views(s, a, z):
            start = max(first for key, first in x_raw if key == s and first <= a)
            return (
                x_grouped[s][:, a:z, :].rearrange("p (c i) j -> p c j i", i=4),
                x_raw[s, start][:, :, a - start : z - start].rearrange("p j (c i) -> p c j i", i=4),
            )

        def w1_views(e, s, a, z):
            return (
                w1_grouped[e, s][:, :, a:z, :].rearrange("p t m j -> p m j t"),
                w1_raw[e, s][:, :, a * PACK : z * PACK].rearrange("p j (m t) -> p m j t", t=PACK),
            )

        def x_cast(s):
            x_grouped[s] = keep.tile([P, T, PACK], BF16, align_bytes=64, name=f"x_grouped{s}")
            for a in (0, T_HALF):
                dst, src = x_views(s, a, a + X_VECTOR)
                nc.vector.tensor_copy(dst, src)
                dst, src = x_views(s, a + X_VECTOR, a + T_HALF)
                nc.scalar.copy(dst, src)

        def x_quantize(s):
            nc.vector.quantize_mx(
                out=x_codes[s][:].bitcast(FP8X4),
                scales=x_scales[s * SCALE_ROW :, :],
                in_=x_grouped[s][:].rearrange("p n j -> p (n j)"),
            )

        def picks(group):
            return offs_t[:, GROUPS[group][0] // 16 : GROUPS[group][1] // 16]

        def gather_words(group, s):
            if s == 0:
                size = GROUPS[group][1] - GROUPS[group][0]
                words[group] = keep.tile(
                    [P, PASSES, size], U32, align_bytes=64, name=f"words{group}", tag=WORD_TAGS[group]
                )
            nc.vector.tensor_copy(words[group][:, s, :], x_codes[s][:].indirect(picks(group)))

        def gather_scales(group):
            size = GROUPS[group][1] - GROUPS[group][0]
            slot_scales[group] = keep.tile(
                [P, size], U8, align_bytes=64, name=f"slot_scales{group}", tag=SCALE_TAGS[group]
            )
            nc.vector.tensor_copy(slot_scales[group][:], x_scales[:].indirect(picks(group)))

        def w1_cast(e, s):
            w1_grouped[e, s] = keep.tile(
                [P, PACK, P, PACK], BF16, align_bytes=64, name=f"w1_grouped{e}_{s}", tag=f"grouped{e}{s}"
            )
            split = W1_VECTOR[e][s]
            if split > 0:
                dst, src = w1_views(e, s, 0, split)
                nc.vector.tensor_copy(dst, src)
            if split < P:
                dst, src = w1_views(e, s, split, P)
                nc.scalar.copy(dst, src)

        def w1_quantize(e, s):
            w1_codes[e, s] = keep.tile([P, H], U32, align_bytes=64, name=f"w1_codes{e}_{s}")
            w1_scales[e, s] = keep.tile([P, H], U8, align_bytes=64, name=f"w1_scales{e}_{s}")
            nc.vector.quantize_mx(
                out=w1_codes[e, s][:].bitcast(FP8X4),
                scales=w1_scales[e, s][:],
                in_=w1_grouped[e, s][:].rearrange("p t m j -> p (t m j)"),
            )

        def w2_cast(e):
            w2_grouped[e] = keep.tile([P, N, PACK], BF16, align_bytes=64, name=f"w2_grouped{e}")
            split = W2_VECTOR[e]
            if split > 0:
                nc.vector.tensor_copy(
                    w2_grouped[e][:, :split, :].rearrange("p (c i) j -> p c j i", i=4),
                    w2_raw[e][:, :, :split].rearrange("p j (c i) -> p c j i", i=4),
                )
            if split < N:
                nc.scalar.copy(
                    w2_grouped[e][:, split:, :].rearrange("p (c i) j -> p c j i", i=4),
                    w2_raw[e][:, :, split:].rearrange("p j (c i) -> p c j i", i=4),
                )

        def w2_quantize(e):
            w2_codes[e] = keep.tile([P, N], U32, align_bytes=64, name=f"w2_codes{e}")
            w2_scales[e] = keep.tile([P, N], U8, align_bytes=64, name=f"w2_scales{e}")
            nc.vector.quantize_mx(
                out=w2_codes[e][:].bitcast(FP8X4), scales=w2_scales[e][:], in_=w2_grouped[e][:].rearrange("p n j -> p (n j)")
            )

        def first_matmul(e):
            for half in range(2):
                slot = e * C + half * HALF
                group = [g for g in range(len(GROUPS)) if GROUPS[g][0] <= slot < GROUPS[g][1]][0]
                cols = slice(slot - GROUPS[group][0], slot - GROUPS[group][0] + HALF)
                acc = psum_h.tile([P, PACK, HALF], F32, name="h_acc")
                for t in range(PACK):
                    rows = slice(t * P, (t + 1) * P)
                    for s in range(PASSES):
                        nc.tensor.matmul_mx(
                            out=acc[:, t, :],
                            lhsT=w1_codes[e, s][:, rows].bitcast(FP8X4),
                            lhsT_scale=w1_scales[e, s][:, rows],
                            rhs=words[group][:, s, cols].bitcast(FP8X4),
                            rhs_scale=slot_scales[group][s * SCALE_ROW :, cols],
                            start=(s == 0),
                            stop=(s == PASSES - 1),
                        )
                h_acc[e, half] = acc

        def h_tile(e, tag):
            h_grouped[e] = keep.tile([P, C, PACK], BF16, align_bytes=64, name=f"h_grouped{e}", tag=tag)

        def relu_scalar(e, half):
            nc.scalar.activation(
                h_grouped[e][:, half * HALF : (half + 1) * HALF, :], h_acc[e, half][:].rearrange("p t n -> p n t"), RELU
            )

        def relu_vector(e, half):
            nc.vector.tensor_scalar_max(
                h_grouped[e][:, half * HALF : (half + 1) * HALF, :], h_acc[e, half][:].rearrange("p t n -> p n t"), 0.0
            )

        def h_quantize(e, a, z):
            if a == 0:
                h_codes[e] = keep.tile([P, C], U32, align_bytes=64, name=f"h_codes{e}")
                h_scales[e] = keep.tile([P, C], U8, align_bytes=64, name=f"h_scales{e}")
            nc.vector.quantize_mx(
                out=h_codes[e][:, a:z].bitcast(FP8X4),
                scales=h_scales[e][:, a:z],
                in_=h_grouped[e][:, a:z, :].rearrange("p n t -> p (n t)"),
            )

        def second_matmul(e, a, z):
            for b in range(N_BLOCKS):
                if (e, b) not in y_acc:
                    y_acc[e, b] = y_acc[0, b] if e == 1 else psum_y.tile([P, 2, C], F32, name="y_acc")
                nc.tensor.matmul_mx(
                    out=y_acc[e, b][:, e % 2, a:z],
                    lhsT=w2_codes[e][:, b * P : (b + 1) * P].bitcast(FP8X4),
                    lhsT_scale=w2_scales[e][:, b * P : (b + 1) * P],
                    rhs=h_codes[e][:, a:z].bitcast(FP8X4),
                    rhs_scale=h_scales[e][:, a:z],
                    start=True,
                    stop=True,
                )

        def y_copy(e, count, b, engine_copy):
            engine_copy(
                y[b][:, e * C : (e + count) * C],
                y_acc[e, b][:, e % 2 : e % 2 + count, :].rearrange("p e n -> p (e n)"),
            )

        nc.gpsimd.memset(x_scales[:], 0)
        identity = keep.tile([P, P], F32, name="identity")
        make_identity(nc, identity[:])

        load_x(0, 0, T_HALF)
        nc.sync.dma_start(out=offs_t[:], in_=offs)
        load_x(0, T_HALF, T)
        load_x(1, 0, T)
        load_w1(0, 0)
        load_w1(0, 1)
        load_w1(1, 0)
        load_w1(1, 1)
        load_w2(0)
        load_w1(2, 0)
        load_w1(2, 1)
        load_w2(2)
        load_w1(3, 0)
        nc.sync.dma_start(out=pos1_t[:], in_=pos1)
        nc.sync.dma_start(out=pos2_t[:], in_=pos2)
        load_w1(3, 1)
        load_w2(1)
        load_w2(3)
        for b in range(N_BLOCKS):
            nc.sync.dma_start(out=gates[b][:], in_=gate[:, b * P : (b + 1) * P, :].rearrange("r p t -> p r t"))

        x_cast(0)
        x_quantize(0)
        x_cast(1)
        gather_words(0, 0)
        x_quantize(1)
        w1_cast(0, 0)
        gather_words(0, 1)
        gather_scales(0)
        w1_quantize(0, 0)
        w1_cast(0, 1)
        gather_words(1, 0)
        w1_quantize(0, 1)
        first_matmul(0)
        w1_cast(1, 0)
        gather_words(1, 1)
        gather_scales(1)
        w1_quantize(1, 0)
        w1_cast(1, 1)
        h_tile(0, "raw11")
        relu_vector(0, 0)
        relu_scalar(0, 1)
        gather_words(2, 0)
        gather_words(2, 1)
        gather_scales(2)
        h_quantize(0, 0, C)
        w1_quantize(1, 1)
        first_matmul(1)
        w2_cast(1)
        w2_quantize(1)
        w2_cast(2)
        w2_quantize(2)
        w1_cast(2, 0)
        w1_quantize(2, 0)
        w1_cast(2, 1)
        h_tile(1, "raw21")
        relu_vector(1, 0)
        relu_scalar(1, 1)
        h_quantize(1, 0, C)
        w1_quantize(2, 1)
        first_matmul(2)
        w2_cast(0)
        w2_quantize(0)
        second_matmul(0, 0, C)
        w1_cast(3, 0)
        w1_quantize(3, 0)
        w1_cast(3, 1)
        h_tile(2, "raw31")
        relu_scalar(2, 0)
        relu_scalar(2, 1)
        h_quantize(2, 0, C)
        w1_quantize(3, 1)
        first_matmul(3)
        w2_cast(3)
        h_tile(3, "h_grouped3")
        relu_scalar(3, 0)
        relu_vector(3, 1)
        second_matmul(1, 0, C)
        y_copy(0, 2, 0, nc.scalar.copy)
        y_copy(0, 2, 1, nc.scalar.copy)
        second_matmul(2, 0, C)
        w2_quantize(3)
        h_quantize(3, 0, HALF)
        second_matmul(3, 0, HALF)
        h_quantize(3, HALF, C)
        second_matmul(3, HALF, C)
        y_copy(2, 1, 0, nc.scalar.copy)
        y_copy(2, 1, 1, nc.scalar.copy)
        y_copy(3, 1, 0, nc.vector.tensor_copy)
        y_copy(3, 1, 1, nc.scalar.copy)

        picked = {}

        def pick(b, r, a, z):
            places = (pos1_t, pos2_t)[r]
            picked[b, r, a] = keep.tile([P, z - a], F32, name=f"picked{b}_{r}_{a}")
            nc.vector.tensor_tensor(
                picked[b, r, a][:], y[b][:].indirect(places[:, a // 16 : z // 16]), gates[b][:, r, a:z], MULT
            )

        pick(0, 0, 0, T)
        pick(0, 1, 0, T)
        total = keep.tile([P, T], F32, name="total0")
        acc = psum_y.tile([P, T], F32, name="y_acc")
        nc.tensor.matmul(acc[:, :PE_SUMS], identity[:], picked[0, 0, 0][:, :PE_SUMS], start=True, stop=False)
        nc.tensor.matmul(acc[:, :PE_SUMS], identity[:], picked[0, 1, 0][:, :PE_SUMS], start=False, stop=True)
        nc.scalar.copy(total[:, :PE_SUMS], acc[:, :PE_SUMS])
        nc.vector.tensor_tensor(
            total[:, PE_SUMS:], picked[0, 0, 0][:, PE_SUMS:], picked[0, 1, 0][:, PE_SUMS:], ADD
        )
        nc.sync.dma_start(out=out[:P, :], in_=total[:])

        pick(1, 0, 0, T)
        halves = ((0, T_HALF), (T_HALF, T))
        for a, z in halves:
            pick(1, 1, a, z)
        for a, z in halves:
            total = keep.tile([P, T_HALF], F32, name=f"total1_{a}")
            nc.vector.tensor_tensor(total[:], picked[1, 0, 0][:, a:z], picked[1, 1, a][:], ADD)
            nc.sync.dma_start(out=out[P:, a:z], in_=total[:])
